import numpy as np
import ml_dtypes


def mxq(x, axis, fmt="e4m3"):
    dtype, down = {"e4m3": (ml_dtypes.float8_e4m3fn, 7), "e5m2": (ml_dtypes.float8_e5m2, 14)}[fmt]
    v = np.moveaxis(np.asarray(x, np.float32).astype(ml_dtypes.bfloat16).astype(np.float64), axis, -1)
    blocks = v.reshape(v.shape[:-1] + (-1, 32))
    amax = np.abs(blocks).max(-1, keepdims=True)
    byte = np.maximum(np.where(amax > 0, np.frexp(amax)[1] - 1 + 127, 0) - down, 1)
    scale = np.exp2(byte - 127.0)
    codes = (blocks / scale).astype(np.float32).astype(dtype).astype(np.float64)
    return np.moveaxis((codes * scale).reshape(v.shape), -1, axis)


WIDE = False


def mx_kscale(k):
    if not WIDE:
        return np.ones(k)
    levels = np.array([10, -10, 5, -5, 0])
    if k % 512:
        return np.exp2(np.random.permutation(np.resize(levels, k // 32))).repeat(32)
    a = np.empty((k // 512, 16))
    for p in range(k // 512):
        a[p, :8] = np.random.permutation(np.resize(levels, 8))
        for g in range(8):
            far = levels[np.abs(levels - a[p, g]) >= 10]
            a[p, g + 8] = far[np.random.randint(len(far))]
    return np.exp2(a.ravel()).repeat(32)


BF16 = ml_dtypes.bfloat16


def bf(x):
    return np.asarray(x, np.float32).astype(BF16)


def f64(x):
    return np.asarray(x).astype(np.float64)


E2M1 = np.array([0.0, 0.5, 1.0, 1.5, 2.0, 3.0, 4.0, 6.0, -0.0, -0.5, -1.0, -1.5, -2.0, -3.0, -4.0, -6.0])


def pack_weight(w, fmt):
    k, n = w.shape
    w = f64(bf(w)).reshape(k // 32, 32, n)
    amax = np.abs(w).max(1)
    if fmt == "e4m3":
        byte = np.frexp(amax)[1] - 1 + 127 - 7
    else:
        mant, ex = np.frexp(amax / 6.0)
        byte = np.where(mant > 0.5, ex, ex - 1) + 127
    byte = np.clip(np.where(amax > 0, byte, 1), 1, 254)
    scaled = (w * np.exp2(127.0 - byte)[:, None, :]).reshape(k, n).astype(np.float32)
    by_word = np.ascontiguousarray(scaled.reshape(k // 512, 128, 4, n).transpose(0, 1, 3, 2))
    if fmt == "e4m3":
        words = by_word.astype(ml_dtypes.float8_e4m3fn).view(np.uint8)
    else:
        c = by_word.astype(ml_dtypes.float4_e2m1fn).view(np.uint8) & 0xF
        words = c[..., 0::2] | (c[..., 1::2] << 4)
    return np.ascontiguousarray(words), np.ascontiguousarray(byte.astype(np.uint8).reshape(k // 512, 16, n))


def unpack_weight(words, scales, fmt):
    g, p, n, _ = words.shape
    if fmt == "e4m3":
        vals = np.ascontiguousarray(words).view(ml_dtypes.float8_e4m3fn).astype(np.float64)
    else:
        nib = np.empty((g, p, n, 4), np.uint8)
        nib[..., 0::2] = words & 0xF
        nib[..., 1::2] = words >> 4
        vals = E2M1[nib]
    vals = vals * np.repeat(np.exp2(scales.astype(np.float64) - 127.0), 8, axis=1)[..., None]
    return vals.transpose(0, 1, 3, 2).reshape(g * 512, n)
def pack4(w):
    words, scales = pack_weight(w, "e2m1")
    return words.reshape(words.shape[0], 128, -1), scales


def unpack4(words, scales):
    return unpack_weight(words.reshape(words.shape[0], 128, -1, 2), scales, "e2m1")


M, K, I, J, O = 1024, 2048, 512, 4, 1024


def setup_inputs():
    s, t = mx_kscale(K), mx_kscale(I)
    e = mx_kscale(I)[::I // J]
    x = np.random.standard_normal((K, M)) * s[:, None]
    u = np.random.standard_normal((K, I)) / np.sqrt(K) / s[:, None] * t
    core = np.random.standard_normal((J, I, O)) / np.sqrt(J * I) / t[:, None] / e[:, None, None]
    x_words, x_scales = pack4(x)
    u_words, u_scales = pack4(u)
    return {"x_words": x_words, "x_scales": x_scales,
            "u_words": u_words, "u_scales": u_scales,
            "b": bf(0.3 * np.random.standard_normal(I) * t),
            "v": bf(np.random.standard_normal((M, J)) * e),
            "core": bf(core)}


def reference(x_words, x_scales, u_words, u_scales, b, v, core):
    x = unpack4(x_words, x_scales)
    u = unpack4(u_words, u_scales)
    h = (x.T @ u) + f64(b)
    z = f64(v)[:, :, None] * h[:, None, :]
    z = z.reshape(M, J * I)
    c = f64(core).reshape(J * I, O)
    return mxq(z, 1, "e4m3") @ mxq(c, 0, "e4m3")

@@ -1,0 +1,317 @@
+from contextlib import ExitStack
+
+import concourse.mybir as mybir
+from concourse.masks import make_identity
+
+M, K, I, J, O = 1024, 2048, 512, 4, 1024
+FLOPS = 2 * M * K * I + 2 * M * J * I * O
+
+F32 = mybir.dt.float32
+BF16 = mybir.dt.bfloat16
+I32 = mybir.dt.int32
+U32 = mybir.dt.uint32
+U8 = mybir.dt.uint8
+FP8X4 = mybir.dt.float8_e4m3fn_x4
+FP4X4 = mybir.dt.float4_e2m1fn_x4
+ALU = mybir.AluOpType
+ACT = mybir.ActivationFunctionType
+
+P = 128
+G = K // 512
+T = 4
+HALF = 512
+RUN = 4
+
+
+def tile_tensor_feature_core_s4_kernel(tc, x_words, x_scales, u_words, u_scales, b, v, core, out):
+    nc = tc.nc
+    with ExitStack() as ctx:
+        sb = ctx.enter_context(tc.tile_pool(name="sb", bufs=1))
+        ps = ctx.enter_context(tc.psum_pool(name="ps", bufs=1))
+        ctx.enter_context(tc.manual_schedule())
+
+        def sbuf(name, shape, dtype, tag=None):
+            return sb.tile(shape, dtype, name=name, tag=tag or name, align_bytes=64)
+
+        def bank(n, name):
+            return ps.tile([P, HALF], F32, name=name, tag="bank%d" % n)
+
+        us_raw = sbuf("us_raw", [P, G, I], U8)
+        xs = sbuf("xs", [P, G, M], U8)
+        nc.vector.memset(us_raw[:].bitcast(I32), 0)
+        nc.vector.memset(xs[:].bitcast(I32), 0)
+
+        b_rows = sbuf("b_rows", [P, P], BF16)
+        v_raw = sbuf("v_raw", [P, 2, RUN * J], BF16)
+        ident = sbuf("ident", [P, P], F32)
+        nc.gpsimd.memset(b_rows[:], 0.0)
+        nc.gpsimd.dma_start(out=v_raw[:], in_=v.rearrange("(h p r) j -> p h (r j)", h=2, r=RUN))
+        nc.gpsimd.dma_start(
+            out=b_rows[0:T, :].rearrange("t (s e) -> t s e", e=4),
+            in_=b.rearrange("(s t e) -> t s e", t=T, e=4),
+        )
+        make_identity(nc, ident[:])
+
+        def load_scales(plane, scales):
+            rows = scales.bitcast(I32)
+            for q in range(4):
+                nc.sync.dma_start(
+                    out=plane[32 * q : 32 * q + 4].bitcast(I32),
+                    in_=rows[:, 4 * q : 4 * q + 4, :].rearrange("g r n -> r g n"),
+                )
+
+        def load_x(m0, w):
+            xw = sbuf("xw%d" % m0, [P, G, 2 * w], U8)
+            nc.sync.dma_start(
+                out=xw[:].bitcast(I32),
+                in_=x_words.bitcast(I32)[:, :, m0 // 2 : (m0 + w) // 2].rearrange("g p n -> p g n"),
+            )
+            return xw
+
+        c_raw = {}
+
+        def load_c(j, oh):
+            raw = sbuf("c_raw%d_%d" % (j, oh), [P, T, HALF], BF16)
+            rows = core[j].rearrange("(s t e) o -> e s t o", t=T, e=4)
+            for e in range(4):
+                nc.sync.dma_start(out=raw[e:P:4], in_=rows[e][:, :, oh * HALF : (oh + 1) * HALF])
+            c_raw[j, oh] = raw
+
+        uw_raw = sbuf("uw_raw", [P, G, 2 * I], U8)
+        nc.sync.dma_start(out=uw_raw[:].bitcast(I32), in_=u_words.bitcast(I32).rearrange("g p n -> p g n"))
+        load_scales(us_raw, u_scales)
+        xw_q0 = load_x(0, 256)
+        load_scales(xs, x_scales)
+        load_c(0, 0)
+        load_c(1, 0)
+        xw_q1 = load_x(256, 256)
+        load_c(2, 0)
+        load_c(3, 0)
+        xw_h1 = load_x(512, 512)
+        for j in range(J):
+            load_c(j, 1)
+
+        b_f32 = sbuf("b_f32", [P, P], F32)
+        nc.scalar.activation(out=b_f32[:], in_=b_rows[:], func=ACT.Identity)
+        v_words = v_raw[:].bitcast(F32)
+        v_bank = {}
+        for h in range(2):
+            for u in range(2):
+                vb = bank(4 + 2 * h + u, "v%d_%d" % (h, u))
+                for r in range(RUN):
+                    col = v_words[:, h, 2 * r + u : 2 * r + u + 1]
+                    nc.tensor.transpose(vb[:, r * P : (r + 1) * P], col.to_broadcast([P, P]), ident[:])
+                v_bank[h, u] = vb
+        b_bank = bank(3, "b_bank")
+        nc.tensor.transpose(b_bank[:, 0:P], b_f32[:], ident[:])
+        b_col = sbuf("b_col", [P, T], F32)
+        nc.scalar.copy(out=b_col[:], in_=b_bank[:, 0:T])
+
+        uw, us = [], []
+        for t in range(T):
+            uw_t = sbuf("uw%d" % t, [P, G, 2 * P], U8)
+            us_t = sbuf("us%d" % t, [P, G, P], U8)
+            nc.vector.tensor_copy(
+                out=uw_t[:].bitcast(I32).rearrange("p g (s w) -> p g s w", w=2),
+                in_=uw_raw[:].bitcast(I32).rearrange("p g (s t w) -> p g s t w", t=T, w=2)[:, :, :, t, :],
+            )
+            nc.vector.tensor_copy(
+                out=us_t[:].bitcast(I32),
+                in_=us_raw[:].bitcast(I32).rearrange("p g (s t) -> p g s t", t=T)[:, :, :, t],
+            )
+            uw.append(uw_t)
+            us.append(us_t)
+
+        def stage1(acc, t, xw, m0, w):
+            for g in range(G):
+                nc.tensor.matmul_mx(
+                    out=acc,
+                    lhsT=uw[t][:, g, :].bitcast(FP4X4),
+                    lhsT_scale=us[t][:, g, :],
+                    rhs=xw[:, g, :].bitcast(FP4X4),
+                    rhs_scale=xs[:, g, m0 : m0 + w],
+                    start=(g == 0),
+                    stop=(g == G - 1),
+                )
+
+        def stage1_quarter(xw, m0, banks):
+            accs = []
+            for half in range(2):
+                pair = bank(banks[half], "h%d_%d" % (m0, half))
+                for tt in range(2):
+                    acc = pair[:, tt * 256 : (tt + 1) * 256]
+                    stage1(acc, 2 * half + tt, xw, m0, 256)
+                    accs.append(acc)
+            return accs
+
+        def bias_vector(hb, t, acc):
+            nc.vector.tensor_scalar(out=hb[:, t, :], in0=acc, scalar1=b_col[:, t : t + 1], scalar2=None, op0=ALU.add)
+
+        def bias_scalar(hb, t, acc):
+            nc.scalar.activation(out=hb[:, t, :], in_=acc, func=ACT.Identity, bias=b_col[:, t : t + 1])
+
+        c_stage = {}
+        c_codes = {}
+
+        def interleave_c(j, oh, engine, tag=None):
+            stage = sbuf("c_stage%d_%d" % (j, oh), [P, HALF * T], BF16, tag)
+            dst = stage[:].rearrange("p (c i t) -> p c t i", i=RUN, t=T)
+            src = c_raw[j, oh][:].rearrange("p t (c i) -> p c t i", i=RUN)
+            if engine == "vector":
+                nc.vector.tensor_copy(out=dst, in_=src)
+            elif engine == "scalar":
+                nc.scalar.copy(out=dst, in_=src)
+            else:
+                dst = stage[:].rearrange("p (c t) -> p c t", t=T)
+                src = c_raw[j, oh][:].rearrange("p t c -> p c t")
+                nc.gpsimd.tensor_scalar(out=dst, in0=src, scalar1=1.0, scalar2=0.0, op0=ALU.mult, op1=ALU.add)
+            c_stage[j, oh] = stage
+
+        def quantize_c(j, oh):
+            codes = sbuf("c_codes%d_%d" % (j, oh), [P, HALF], U32)
+            scales = sbuf("c_scales%d_%d" % (j, oh), [P, HALF], U8)
+            nc.vector.quantize_mx(out=codes[:].bitcast(FP8X4), scales=scales[:], in_=c_stage[j, oh][:])
+            c_codes[j, oh] = (codes, scales)
+
+        z_stage = {}
+        z_codes = {}
+
+        def multiply(hb, hb_m0, m0, w, j, group):
+            key = (m0, group[0])
+            if key not in z_stage:
+                z_stage[key] = sbuf("z_stage%d_%d" % key, [P, len(group) * w * T], BF16)
+            n = j - group[0]
+            dst = z_stage[key][:, n * w * T : (n + 1) * w * T].rearrange("p (c i t) -> p c t i", i=RUN, t=T)
+            src = hb[:, :, m0 - hb_m0 : m0 - hb_m0 + w].rearrange("p t (c i) -> p c t i", i=RUN)
+            c0 = (m0 % HALF) // RUN
+            vj = v_bank[m0 // HALF, j // 2][:].bitcast(BF16).rearrange("p (r c e) -> p c e r", r=RUN, e=2)
+            vj = vj[:, c0 : c0 + w // RUN, j % 2 : j % 2 + 1, :].broadcast_to([P, w // RUN, T, RUN])
+            nc.vector.tensor_tensor(out=dst, in0=src, in1=vj, op=ALU.mult)
+
+        def quantize_z(m0, w, group):
+            key = (m0, group[0])
+            codes = sbuf("z_codes%d_%d" % key, [P, len(group) * w], U32)
+            scales = sbuf("z_scales%d_%d" % key, [P, len(group) * w], U8)
+            nc.vector.quantize_mx(out=codes[:].bitcast(FP8X4), scales=scales[:], in_=z_stage[key][:])
+            for n, j in enumerate(group):
+                for a in range(w // P):
+                    cols = slice(n * w + a * P, n * w + (a + 1) * P)
+                    z_codes[m0 // P + a, j] = (codes[:, cols], scales[:, cols])
+
+        y_acc = {}
+        y_passes = {}
+
+        def stage2(groups, js):
+            for j in js:
+                for mt, oh in groups:
+                    if (mt, oh) not in y_acc:
+                        y_acc[mt, oh] = bank(len(y_acc) % 6, "y%d_%d" % (mt, oh))
+                        y_passes[mt, oh] = 0
+                    done = y_passes[mt, oh]
+                    nc.tensor.matmul_mx(
+                        out=y_acc[mt, oh][:],
+                        lhsT=z_codes[mt, j][0].bitcast(FP8X4),
+                        lhsT_scale=z_codes[mt, j][1],
+                        rhs=c_codes[j, oh][0][:].bitcast(FP8X4),
+                        rhs_scale=c_codes[j, oh][1][:],
+                        start=(done == 0),
+                        stop=(done == J - 1),
+                    )
+                    y_passes[mt, oh] = done + 1
+
+        def store(mt, oh, engine="scalar"):
+            y = sbuf("y_sb%d_%d" % (mt, oh), [P, HALF], F32)
+            if engine == "scalar":
+                nc.scalar.copy(out=y[:], in_=y_acc[mt, oh][:])
+            else:
+                nc.vector.tensor_copy(out=y[:], in_=y_acc[mt, oh][:])
+            nc.sync.dma_start(out=out[mt * P : (mt + 1) * P, oh * HALF : (oh + 1) * HALF], in_=y[:])
+
+        ALL, LOW, HIGH = (0, 1, 2, 3), (0, 1), (2, 3)
+        hb0 = sbuf("hb0", [P, T, 256], F32)
+        hb1 = sbuf("hb1", [P, T, 256], F32)
+        hb2 = sbuf("hb2", [P, T, HALF], F32)
+
+        h0 = stage1_quarter(xw_q0, 0, (0, 1))
+        h1 = stage1_quarter(xw_q1, 256, (2, 3))
+        interleave_c(0, 0, "vector", "shared_stage")
+        bias_vector(hb0, 0, h0[0])
+        bias_vector(hb0, 1, h0[1])
+        quantize_c(0, 0)
+        bias_vector(hb0, 2, h0[2])
+        bias_vector(hb0, 3, h0[3])
+        interleave_c(2, 0, "gpsimd", "shared_stage")
+        interleave_c(1, 0, "scalar")
+        interleave_c(3, 0, "scalar")
+        for t in range(T):
+            bias_scalar(hb1, t, h1[t])
+        h2 = []
+        for t in range(T):
+            acc = bank(t, "h512_%d" % t)
+            stage1(acc[:], t, xw_h1, HALF, HALF)
+            h2.append(acc)
+
+        for j in ALL:
+            multiply(hb0, 0, 0, 256, j, ALL)
+        quantize_c(1, 0)
+        quantize_z(0, 256, ALL)
+        quantize_c(3, 0)
+        quantize_c(2, 0)
+        interleave_c(0, 1, "gpsimd", "shared_stage")
+        interleave_c(1, 1, "scalar")
+        for t in range(T):
+            bias_scalar(hb2, t, h2[t][:])
+        stage2([(0, 0), (1, 0)], (0, 1, 3, 2))
+        interleave_c(2, 1, "scalar")
+        store(0, 0)
+        store(1, 0)
+        interleave_c(3, 1, "scalar")
+
+        for j in ALL:
+            multiply(hb1, 256, 256, 256, j, ALL)
+        quantize_c(1, 1)
+        quantize_z(256, 256, ALL)
+        quantize_c(0, 1)
+        quantize_c(2, 1)
+        stage2([(2, 0), (3, 0)], ALL)
+        late = [(mt, 1) for mt in range(4)]
+        stage2(late, (1, 0, 2))
+        store(2, 0)
+        store(3, 0)
+
+        multiply(hb2, HALF, 512, 256, 0, LOW)
+        multiply(hb2, HALF, 512, 256, 1, LOW)
+        quantize_c(3, 1)
+        stage2(late, (3,))
+        for mt, oh in late:
+            store(mt, oh)
+        multiply(hb2, HALF, 512, 256, 2, HIGH)
+        quantize_z(512, 256, LOW)
+        third = [(4, 0), (5, 0), (4, 1), (5, 1)]
+        stage2(third, LOW)
+        multiply(hb2, HALF, 512, 256, 3, HIGH)
+        multiply(hb2, HALF, 768, P, 0, LOW)
+        quantize_z(512, 256, HIGH)
+        stage2(third, HIGH)
+        for mt, oh in third:
+            store(mt, oh)
+        multiply(hb2, HALF, 768, P, 1, LOW)
+        multiply(hb2, HALF, 768, P, 2, HIGH)
+        quantize_z(768, P, LOW)
+        stage2([(6, 0), (6, 1)], LOW)
+        multiply(hb2, HALF, 768, P, 3, HIGH)
+        multiply(hb2, HALF, 896, P, 0, LOW)
+        quantize_z(768, P, HIGH)
+        stage2([(6, 0), (6, 1)], HIGH)
+        store(6, 0)
+        store(6, 1)
+        multiply(hb2, HALF, 896, P, 1, LOW)
+        multiply(hb2, HALF, 896, P, 2, (2,))
+        quantize_z(896, P, LOW)
+        stage2([(7, 0), (7, 1)], LOW)
+        multiply(hb2, HALF, 896, P, 3, (3,))
+        quantize_z(896, P, (2,))
+        quantize_z(896, P, (3,))
+        stage2([(7, 0), (7, 1)], HIGH)
+        store(7, 0)
+        store(7, 1, "vector")

@@ -21,6 +21,9 @@ G = K // 512
 T = 4
 HALF = 512
 RUN = 4
+E = 2
+R = 2
+QUARTER = 256
 
 
 def tile_tensor_feature_core_s4_kernel(tc, x_words, x_scales, u_words, u_scales, b, v, core, out):
@@ -42,22 +45,17 @@ def tile_tensor_feature_core_s4_kernel(tc, x_words, x_scales, u_words, u_scales,
         nc.vector.memset(xs[:].bitcast(I32), 0)
 
         b_rows = sbuf("b_rows", [P, P], BF16)
-        v_raw = sbuf("v_raw", [P, 2, RUN * J], BF16)
+        v_raw = sbuf("v_raw", [P, 4, R * J], BF16)
         ident = sbuf("ident", [P, P], F32)
         nc.gpsimd.memset(b_rows[:], 0.0)
-        nc.gpsimd.dma_start(out=v_raw[:], in_=v.rearrange("(h p r) j -> p h (r j)", h=2, r=RUN))
-        nc.gpsimd.dma_start(
-            out=b_rows[0:T, :].rearrange("t (s e) -> t s e", e=4),
-            in_=b.rearrange("(s t e) -> t s e", t=T, e=4),
-        )
         make_identity(nc, ident[:])
 
-        def load_scales(plane, scales):
+        def load_scales(plane, scales, n0, n1):
             rows = scales.bitcast(I32)
             for q in range(4):
                 nc.sync.dma_start(
-                    out=plane[32 * q : 32 * q + 4].bitcast(I32),
-                    in_=rows[:, 4 * q : 4 * q + 4, :].rearrange("g r n -> r g n"),
+                    out=plane[32 * q : 32 * q + 4].bitcast(I32)[:, :, n0 // 4 : n1 // 4],
+                    in_=rows[:, 4 * q : 4 * q + 4, n0 // 4 : n1 // 4].rearrange("g r n -> r g n"),
                 )
 
         def load_x(m0, w):
@@ -72,37 +70,49 @@ def tile_tensor_feature_core_s4_kernel(tc, x_words, x_scales, u_words, u_scales,
 
         def load_c(j, oh):
             raw = sbuf("c_raw%d_%d" % (j, oh), [P, T, HALF], BF16)
-            rows = core[j].rearrange("(s t e) o -> e s t o", t=T, e=4)
-            for e in range(4):
-                nc.sync.dma_start(out=raw[e:P:4], in_=rows[e][:, :, oh * HALF : (oh + 1) * HALF])
+            rows = core[j].rearrange("(s t e) o -> e s t o", t=T, e=E)
+            for e in range(E):
+                nc.sync.dma_start(out=raw[e:P:E], in_=rows[e][:, :, oh * HALF : (oh + 1) * HALF])
             c_raw[j, oh] = raw
 
+        nc.sync.dma_start(out=v_raw[:], in_=v.rearrange("(q p r) j -> p q (r j)", q=4, r=R))
+        nc.sync.dma_start(
+            out=b_rows[0:T, :].rearrange("t (s e) -> t s e", e=E),
+            in_=b.rearrange("(s t e) -> t s e", t=T, e=E),
+        )
+        load_scales(us_raw, u_scales, 0, I)
         uw_raw = sbuf("uw_raw", [P, G, 2 * I], U8)
         nc.sync.dma_start(out=uw_raw[:].bitcast(I32), in_=u_words.bitcast(I32).rearrange("g p n -> p g n"))
-        load_scales(us_raw, u_scales)
         xw_q0 = load_x(0, 256)
-        load_scales(xs, x_scales)
+        load_scales(xs, x_scales, 0, QUARTER)
         load_c(0, 0)
         load_c(1, 0)
+        load_scales(xs, x_scales, QUARTER, M)
         xw_q1 = load_x(256, 256)
         load_c(2, 0)
+        load_c(0, 1)
         load_c(3, 0)
         xw_h1 = load_x(512, 512)
-        for j in range(J):
+        for j in (1, 3, 2):
             load_c(j, 1)
 
         b_f32 = sbuf("b_f32", [P, P], F32)
         nc.scalar.activation(out=b_f32[:], in_=b_rows[:], func=ACT.Identity)
         v_words = v_raw[:].bitcast(F32)
         v_bank = {}
-        for h in range(2):
+
+        def spread_v(q, n):
+            vb = bank(n, "v%d" % q)
             for u in range(2):
-                vb = bank(4 + 2 * h + u, "v%d_%d" % (h, u))
-                for r in range(RUN):
-                    col = v_words[:, h, 2 * r + u : 2 * r + u + 1]
-                    nc.tensor.transpose(vb[:, r * P : (r + 1) * P], col.to_broadcast([P, P]), ident[:])
-                v_bank[h, u] = vb
-        b_bank = bank(3, "b_bank")
+                for r in range(R):
+                    col = v_words[:, q, 2 * r + u : 2 * r + u + 1]
+                    slot = R * u + r
+                    nc.tensor.transpose(vb[:, slot * P : (slot + 1) * P], col.to_broadcast([P, P]), ident[:])
+            v_bank[q] = vb
+
+        spread_v(0, 4)
+        spread_v(1, 5)
+        b_bank = bank(7, "b_bank")
         nc.tensor.transpose(b_bank[:, 0:P], b_f32[:], ident[:])
         b_col = sbuf("b_col", [P, T], F32)
         nc.scalar.copy(out=b_col[:], in_=b_bank[:, 0:T])
@@ -112,35 +122,35 @@ def tile_tensor_feature_core_s4_kernel(tc, x_words, x_scales, u_words, u_scales,
             uw_t = sbuf("uw%d" % t, [P, G, 2 * P], U8)
             us_t = sbuf("us%d" % t, [P, G, P], U8)
             nc.vector.tensor_copy(
-                out=uw_t[:].bitcast(I32).rearrange("p g (s w) -> p g s w", w=2),
-                in_=uw_raw[:].bitcast(I32).rearrange("p g (s t w) -> p g s t w", t=T, w=2)[:, :, :, t, :],
+                out=uw_t[:].bitcast(I32),
+                in_=uw_raw[:].bitcast(I32).rearrange("p g (s t) -> p g s t", t=T)[:, :, :, t],
             )
             nc.vector.tensor_copy(
-                out=us_t[:].bitcast(I32),
-                in_=us_raw[:].bitcast(I32).rearrange("p g (s t) -> p g s t", t=T)[:, :, :, t],
+                out=us_t[:].rearrange("p g (s e) -> p g s e", e=E),
+                in_=us_raw[:].rearrange("p g (s t e) -> p g s t e", t=T, e=E)[:, :, :, t, :],
             )
             uw.append(uw_t)
             us.append(us_t)
 
-        def stage1(acc, t, xw, m0, w):
+        def stage1(acc, t, xw, m0, w, x0=0):
             for g in range(G):
                 nc.tensor.matmul_mx(
                     out=acc,
                     lhsT=uw[t][:, g, :].bitcast(FP4X4),
                     lhsT_scale=us[t][:, g, :],
-                    rhs=xw[:, g, :].bitcast(FP4X4),
+                    rhs=xw[:, g, 2 * x0 : 2 * (x0 + w)].bitcast(FP4X4),
                     rhs_scale=xs[:, g, m0 : m0 + w],
                     start=(g == 0),
                     stop=(g == G - 1),
                 )
 
-        def stage1_quarter(xw, m0, banks):
+        def stage1_pairs(xw, m0, w, banks):
             accs = []
             for half in range(2):
                 pair = bank(banks[half], "h%d_%d" % (m0, half))
                 for tt in range(2):
-                    acc = pair[:, tt * 256 : (tt + 1) * 256]
-                    stage1(acc, 2 * half + tt, xw, m0, 256)
+                    acc = pair[:, tt * w : (tt + 1) * w]
+                    stage1(acc, 2 * half + tt, xw, m0, w, m0 % QUARTER)
                     accs.append(acc)
             return accs
 
@@ -181,11 +191,11 @@ def tile_tensor_feature_core_s4_kernel(tc, x_words, x_scales, u_words, u_scales,
             if key not in z_stage:
                 z_stage[key] = sbuf("z_stage%d_%d" % key, [P, len(group) * w * T], BF16)
             n = j - group[0]
-            dst = z_stage[key][:, n * w * T : (n + 1) * w * T].rearrange("p (c i t) -> p c t i", i=RUN, t=T)
-            src = hb[:, :, m0 - hb_m0 : m0 - hb_m0 + w].rearrange("p t (c i) -> p c t i", i=RUN)
-            c0 = (m0 % HALF) // RUN
-            vj = v_bank[m0 // HALF, j // 2][:].bitcast(BF16).rearrange("p (r c e) -> p c e r", r=RUN, e=2)
-            vj = vj[:, c0 : c0 + w // RUN, j % 2 : j % 2 + 1, :].broadcast_to([P, w // RUN, T, RUN])
+            dst = z_stage[key][:, n * w * T : (n + 1) * w * T].rearrange("p (c i t) -> p c t i", i=R, t=T)
+            src = hb[:, :, m0 - hb_m0 : m0 - hb_m0 + w].rearrange("p t (c i) -> p c t i", i=R)
+            c0 = (m0 % QUARTER) // R
+            vj = v_bank[m0 // QUARTER][:].bitcast(BF16).rearrange("p (u r c e) -> p u c e r", u=2, r=R, e=2)
+            vj = vj[:, j // 2, c0 : c0 + w // R, j % 2 : j % 2 + 1, :].broadcast_to([P, w // R, T, R])
             nc.vector.tensor_tensor(out=dst, in0=src, in1=vj, op=ALU.mult)
 
         def quantize_z(m0, w, group):
@@ -201,11 +211,11 @@ def tile_tensor_feature_core_s4_kernel(tc, x_words, x_scales, u_words, u_scales,
         y_acc = {}
         y_passes = {}
 
-        def stage2(groups, js):
+        def stage2(groups, js, banks=()):
             for j in js:
-                for mt, oh in groups:
+                for n, (mt, oh) in enumerate(groups):
                     if (mt, oh) not in y_acc:
-                        y_acc[mt, oh] = bank(len(y_acc) % 6, "y%d_%d" % (mt, oh))
+                        y_acc[mt, oh] = bank(banks[n], "y%d_%d" % (mt, oh))
                         y_passes[mt, oh] = 0
                     done = y_passes[mt, oh]
                     nc.tensor.matmul_mx(
@@ -228,67 +238,88 @@ def tile_tensor_feature_core_s4_kernel(tc, x_words, x_scales, u_words, u_scales,
             nc.sync.dma_start(out=out[mt * P : (mt + 1) * P, oh * HALF : (oh + 1) * HALF], in_=y[:])
 
         ALL, LOW, HIGH = (0, 1, 2, 3), (0, 1), (2, 3)
-        hb0 = sbuf("hb0", [P, T, 256], F32)
+        hbA = sbuf("hbA", [P, T, P], F32)
+        hbB = sbuf("hbB", [P, T, P], F32)
         hb1 = sbuf("hb1", [P, T, 256], F32)
         hb2 = sbuf("hb2", [P, T, HALF], F32)
 
-        h0 = stage1_quarter(xw_q0, 0, (0, 1))
-        h1 = stage1_quarter(xw_q1, 256, (2, 3))
+        hA = stage1_pairs(xw_q0, 0, P, (0, 1))
+        hB = stage1_pairs(xw_q0, P, P, (2, 3))
         interleave_c(0, 0, "vector", "shared_stage")
-        bias_vector(hb0, 0, h0[0])
-        bias_vector(hb0, 1, h0[1])
+        bias_scalar(hbA, 0, hA[0])
+        bias_scalar(hbA, 1, hA[1])
+        bias_vector(hbA, 2, hA[2])
+        bias_vector(hbA, 3, hA[3])
         quantize_c(0, 0)
-        bias_vector(hb0, 2, h0[2])
-        bias_vector(hb0, 3, h0[3])
         interleave_c(2, 0, "gpsimd", "shared_stage")
+        interleave_c(0, 1, "gpsimd")
+        h1 = stage1_pairs(xw_q1, 256, 256, (0, 1))
         interleave_c(1, 0, "scalar")
-        interleave_c(3, 0, "scalar")
+        for t in range(T):
+            bias_scalar(hbB, t, hB[t])
         for t in range(T):
             bias_scalar(hb1, t, h1[t])
+        interleave_c(3, 0, "scalar")
         h2 = []
         for t in range(T):
-            acc = bank(t, "h512_%d" % t)
+            acc = bank((6, 7, 2, 3)[t], "h512_%d" % t)
             stage1(acc[:], t, xw_h1, HALF, HALF)
             h2.append(acc)
 
         for j in ALL:
-            multiply(hb0, 0, 0, 256, j, ALL)
-        quantize_c(1, 0)
-        quantize_z(0, 256, ALL)
-        quantize_c(3, 0)
-        quantize_c(2, 0)
-        interleave_c(0, 1, "gpsimd", "shared_stage")
+            multiply(hbA, 0, 0, P, j, ALL)
+        for j in ALL:
+            multiply(hbB, P, P, P, j, ALL)
+        multiply(hb1, 256, 256, 256, 0, (0,))
         interleave_c(1, 1, "scalar")
+        quantize_z(0, P, ALL)
+        quantize_c(1, 0)
+        quantize_c(0, 1)
+        stage2([(0, 0)], LOW, [0])
+        stage2([(0, 1)], (0,), [4])
+        quantize_z(P, P, ALL)
+        stage2([(1, 0)], LOW, [1])
+        quantize_c(3, 0)
+        stage2([(0, 0), (1, 0)], (3,))
+        quantize_z(256, 256, (0,))
+        quantize_c(1, 1)
+        quantize_c(2, 0)
+        interleave_c(2, 1, "gpsimd", "shared_stage")
         for t in range(T):
             bias_scalar(hb2, t, h2[t][:])
-        stage2([(0, 0), (1, 0)], (0, 1, 3, 2))
-        interleave_c(2, 1, "scalar")
+        interleave_c(3, 1, "scalar")
+        stage2([(0, 1)], (1,))
+        stage2([(0, 0), (1, 0)], (2,))
+        spread_v(2, 6)
+        spread_v(3, 7)
+        stage2([(1, 1)], LOW, [2])
+        stage2([(2, 0)], (0,), [3])
         store(0, 0)
         store(1, 0)
-        interleave_c(3, 1, "scalar")
-
-        for j in ALL:
-            multiply(hb1, 256, 256, 256, j, ALL)
-        quantize_c(1, 1)
-        quantize_z(256, 256, ALL)
-        quantize_c(0, 1)
-        quantize_c(2, 1)
-        stage2([(2, 0), (3, 0)], ALL)
-        late = [(mt, 1) for mt in range(4)]
-        stage2(late, (1, 0, 2))
+        stage2([(3, 0), (2, 1)], (0,), [0, 1])
+        multiply(hb1, 256, 256, 256, 1, (1, 2))
+        multiply(hb1, 256, 256, 256, 2, (1, 2))
+        multiply(hb1, 256, 256, 256, 3, (3,))
+        quantize_z(256, 256, (1, 2))
+        stage2([(2, 0), (3, 0)], (1, 2))
+        stage2([(2, 1)], (1,))
+        quantize_z(256, 256, (3,))
+        stage2([(2, 0), (3, 0)], (3,))
+        stage2([(3, 1)], LOW, [5])
         store(2, 0)
         store(3, 0)
-
-        multiply(hb2, HALF, 512, 256, 0, LOW)
-        multiply(hb2, HALF, 512, 256, 1, LOW)
         quantize_c(3, 1)
-        stage2(late, (3,))
+        quantize_c(2, 1)
+        late = [(mt, 1) for mt in range(4)]
+        stage2(late, (3, 2))
         for mt, oh in late:
             store(mt, oh)
+        multiply(hb2, HALF, 512, 256, 0, LOW)
+        multiply(hb2, HALF, 512, 256, 1, LOW)
         multiply(hb2, HALF, 512, 256, 2, HIGH)
         quantize_z(512, 256, LOW)
         third = [(4, 0), (5, 0), (4, 1), (5, 1)]
-        stage2(third, LOW)
+        stage2(third, LOW, [3, 0, 4, 2])
         multiply(hb2, HALF, 512, 256, 3, HIGH)
         multiply(hb2, HALF, 768, P, 0, LOW)
         quantize_z(512, 256, HIGH)
@@ -298,7 +329,7 @@ def tile_tensor_feature_core_s4_kernel(tc, x_words, x_scales, u_words, u_scales,
         multiply(hb2, HALF, 768, P, 1, LOW)
         multiply(hb2, HALF, 768, P, 2, HIGH)
         quantize_z(768, P, LOW)
-        stage2([(6, 0), (6, 1)], LOW)
+        stage2([(6, 0), (6, 1)], LOW, [1, 5])
         multiply(hb2, HALF, 768, P, 3, HIGH)
         multiply(hb2, HALF, 896, P, 0, LOW)
         quantize_z(768, P, HIGH)
@@ -308,7 +339,7 @@ def tile_tensor_feature_core_s4_kernel(tc, x_words, x_scales, u_words, u_scales,
         multiply(hb2, HALF, 896, P, 1, LOW)
         multiply(hb2, HALF, 896, P, 2, (2,))
         quantize_z(896, P, LOW)
-        stage2([(7, 0), (7, 1)], LOW)
+        stage2([(7, 0), (7, 1)], LOW, [6, 3])
         multiply(hb2, HALF, 896, P, 3, (3,))
         quantize_z(896, P, (2,))
         quantize_z(896, P, (3,))

@@ -40,11 +40,13 @@ def tile_tensor_feature_core_s4_kernel(tc, x_words, x_scales, u_words, u_scales,
             return ps.tile([P, HALF], F32, name=name, tag="bank%d" % n)
 
         us_raw = sbuf("us_raw", [P, G, I], U8)
-        xs = sbuf("xs", [P, G, M], U8)
+        xs_first = sbuf("xs_first", [P, G, QUARTER], U8)
+        xs_rest = sbuf("xs_rest", [P, G, M - QUARTER], U8)
         nc.vector.memset(us_raw[:].bitcast(I32), 0)
-        nc.vector.memset(xs[:].bitcast(I32), 0)
+        nc.vector.memset(xs_first[:].bitcast(I32), 0)
+        nc.vector.memset(xs_rest[:].bitcast(I32), 0)
 
-        b_rows = sbuf("b_rows", [P, P], BF16)
+        b_rows = sbuf("b_rows", [P, I], BF16)
         v_raw = sbuf("v_raw", [P, 4, R * J], BF16)
         ident = sbuf("ident", [P, P], F32)
         nc.gpsimd.memset(b_rows[:], 0.0)
@@ -52,10 +54,10 @@ def tile_tensor_feature_core_s4_kernel(tc, x_words, x_scales, u_words, u_scales,
 
         def load_scales(plane, scales, n0, n1):
             rows = scales.bitcast(I32)
-            for q in range(4):
+            for r in range(4):
                 nc.sync.dma_start(
-                    out=plane[32 * q : 32 * q + 4].bitcast(I32)[:, :, n0 // 4 : n1 // 4],
-                    in_=rows[:, 4 * q : 4 * q + 4, n0 // 4 : n1 // 4].rearrange("g r n -> r g n"),
+                    out=plane[r:P:32].bitcast(I32),
+                    in_=rows[:, r:16:4, n0 // 4 : n1 // 4].rearrange("g q n -> q g n"),
                 )
 
         def load_x(m0, w):
@@ -76,28 +78,28 @@ def tile_tensor_feature_core_s4_kernel(tc, x_words, x_scales, u_words, u_scales,
             c_raw[j, oh] = raw
 
         nc.sync.dma_start(out=v_raw[:], in_=v.rearrange("(q p r) j -> p q (r j)", q=4, r=R))
-        nc.sync.dma_start(
-            out=b_rows[0:T, :].rearrange("t (s e) -> t s e", e=E),
-            in_=b.rearrange("(s t e) -> t s e", t=T, e=E),
-        )
-        load_scales(us_raw, u_scales, 0, I)
         uw_raw = sbuf("uw_raw", [P, G, 2 * I], U8)
         nc.sync.dma_start(out=uw_raw[:].bitcast(I32), in_=u_words.bitcast(I32).rearrange("g p n -> p g n"))
+        nc.sync.dma_start(out=b_rows[0:1, :], in_=b.rearrange("(o i) -> o i", o=1))
+        load_scales(us_raw, u_scales, 0, I)
         xw_q0 = load_x(0, 256)
-        load_scales(xs, x_scales, 0, QUARTER)
+        load_scales(xs_first, x_scales, 0, QUARTER)
         load_c(0, 0)
         load_c(1, 0)
-        load_scales(xs, x_scales, QUARTER, M)
+        load_scales(xs_rest, x_scales, QUARTER, M)
         xw_q1 = load_x(256, 256)
         load_c(2, 0)
-        load_c(0, 1)
-        load_c(3, 0)
         xw_h1 = load_x(512, 512)
-        for j in (1, 3, 2):
+        load_c(3, 0)
+        for j in range(J):
             load_c(j, 1)
 
-        b_f32 = sbuf("b_f32", [P, P], F32)
-        nc.scalar.activation(out=b_f32[:], in_=b_rows[:], func=ACT.Identity)
+        b_f32 = sbuf("b_f32", [P, T, P], F32)
+        nc.scalar.activation(
+            out=b_f32[:].rearrange("p t (s e) -> p t s e", e=E),
+            in_=b_rows[:].rearrange("p (s t e) -> p t s e", t=T, e=E),
+            func=ACT.Identity,
+        )
         v_words = v_raw[:].bitcast(F32)
         v_bank = {}
 
@@ -111,11 +113,11 @@ def tile_tensor_feature_core_s4_kernel(tc, x_words, x_scales, u_words, u_scales,
             v_bank[q] = vb
 
         spread_v(0, 4)
-        spread_v(1, 5)
         b_bank = bank(7, "b_bank")
-        nc.tensor.transpose(b_bank[:, 0:P], b_f32[:], ident[:])
+        for t in range(T):
+            nc.tensor.transpose(b_bank[:, t * P : (t + 1) * P], b_f32[:, t, :], ident[:])
         b_col = sbuf("b_col", [P, T], F32)
-        nc.scalar.copy(out=b_col[:], in_=b_bank[:, 0:T])
+        nc.scalar.copy(out=b_col[:], in_=b_bank[:].rearrange("p (t n) -> p t n", t=T)[:, :, 0])
 
         uw, us = [], []
         for t in range(T):
@@ -133,13 +135,14 @@ def tile_tensor_feature_core_s4_kernel(tc, x_words, x_scales, u_words, u_scales,
             us.append(us_t)
 
         def stage1(acc, t, xw, m0, w, x0=0):
+            xs, s0 = (xs_first, m0) if m0 < QUARTER else (xs_rest, m0 - QUARTER)
             for g in range(G):
                 nc.tensor.matmul_mx(
                     out=acc,
                     lhsT=uw[t][:, g, :].bitcast(FP4X4),
                     lhsT_scale=us[t][:, g, :],
                     rhs=xw[:, g, 2 * x0 : 2 * (x0 + w)].bitcast(FP4X4),
-                    rhs_scale=xs[:, g, m0 : m0 + w],
+                    rhs_scale=xs[:, g, s0 : s0 + w],
                     start=(g == 0),
                     stop=(g == G - 1),
                 )
@@ -252,7 +255,7 @@ def tile_tensor_feature_core_s4_kernel(tc, x_words, x_scales, u_words, u_scales,
         bias_vector(hbA, 3, hA[3])
         quantize_c(0, 0)
         interleave_c(2, 0, "gpsimd", "shared_stage")
-        interleave_c(0, 1, "gpsimd")
+        spread_v(1, 5)
         h1 = stage1_pairs(xw_q1, 256, 256, (0, 1))
         interleave_c(1, 0, "scalar")
         for t in range(T):
@@ -270,56 +273,50 @@ def tile_tensor_feature_core_s4_kernel(tc, x_words, x_scales, u_words, u_scales,
             multiply(hbA, 0, 0, P, j, ALL)
         for j in ALL:
             multiply(hbB, P, P, P, j, ALL)
-        multiply(hb1, 256, 256, 256, 0, (0,))
-        interleave_c(1, 1, "scalar")
         quantize_z(0, P, ALL)
         quantize_c(1, 0)
-        quantize_c(0, 1)
         stage2([(0, 0)], LOW, [0])
-        stage2([(0, 1)], (0,), [4])
         quantize_z(P, P, ALL)
         stage2([(1, 0)], LOW, [1])
         quantize_c(3, 0)
-        stage2([(0, 0), (1, 0)], (3,))
-        quantize_z(256, 256, (0,))
-        quantize_c(1, 1)
         quantize_c(2, 0)
-        interleave_c(2, 1, "gpsimd", "shared_stage")
+        interleave_c(0, 1, "gpsimd", "shared_stage")
+        stage2([(0, 0), (1, 0)], (3, 2))
+        interleave_c(1, 1, "scalar")
         for t in range(T):
             bias_scalar(hb2, t, h2[t][:])
-        interleave_c(3, 1, "scalar")
-        stage2([(0, 1)], (1,))
-        stage2([(0, 0), (1, 0)], (2,))
         spread_v(2, 6)
         spread_v(3, 7)
-        stage2([(1, 1)], LOW, [2])
-        stage2([(2, 0)], (0,), [3])
         store(0, 0)
         store(1, 0)
-        stage2([(3, 0), (2, 1)], (0,), [0, 1])
-        multiply(hb1, 256, 256, 256, 1, (1, 2))
-        multiply(hb1, 256, 256, 256, 2, (1, 2))
-        multiply(hb1, 256, 256, 256, 3, (3,))
-        quantize_z(256, 256, (1, 2))
-        stage2([(2, 0), (3, 0)], (1, 2))
-        stage2([(2, 1)], (1,))
-        quantize_z(256, 256, (3,))
-        stage2([(2, 0), (3, 0)], (3,))
-        stage2([(3, 1)], LOW, [5])
-        store(2, 0)
-        store(3, 0)
-        quantize_c(3, 1)
-        quantize_c(2, 1)
-        late = [(mt, 1) for mt in range(4)]
-        stage2(late, (3, 2))
-        for mt, oh in late:
-            store(mt, oh)
+        interleave_c(3, 1, "scalar")
+        multiply(hb1, 256, 256, 256, 0, LOW)
+        multiply(hb1, 256, 256, 256, 1, LOW)
+        multiply(hb1, 256, 256, 256, 2, HIGH)
+        quantize_z(256, 256, LOW)
+        stage2([(2, 0), (3, 0)], LOW, [4, 2])
+        quantize_c(1, 1)
+        quantize_c(0, 1)
+        interleave_c(2, 1, "gpsimd", "shared_stage")
+        stage2([(0, 1), (1, 1), (2, 1)], (1, 0), [3, 0, 1])
+        multiply(hb1, 256, 256, 256, 3, HIGH)
         multiply(hb2, HALF, 512, 256, 0, LOW)
         multiply(hb2, HALF, 512, 256, 1, LOW)
-        multiply(hb2, HALF, 512, 256, 2, HIGH)
+        quantize_z(256, 256, HIGH)
+        stage2([(3, 1)], LOW, [5])
+        stage2([(2, 0), (3, 0)], HIGH)
+        store(2, 0)
+        store(3, 0)
+        quantize_c(2, 1)
+        quantize_c(3, 1)
+        late = [(mt, 1) for mt in range(4)]
+        stage2(late, HIGH)
+        for mt, oh in late:
+            store(mt, oh)
         quantize_z(512, 256, LOW)
         third = [(4, 0), (5, 0), (4, 1), (5, 1)]
-        stage2(third, LOW, [3, 0, 4, 2])
+        stage2(third, LOW, [4, 2, 3, 0])
+        multiply(hb2, HALF, 512, 256, 2, HIGH)
         multiply(hb2, HALF, 512, 256, 3, HIGH)
         multiply(hb2, HALF, 768, P, 0, LOW)
         quantize_z(512, 256, HIGH)
@@ -331,18 +328,16 @@ def tile_tensor_feature_core_s4_kernel(tc, x_words, x_scales, u_words, u_scales,
         quantize_z(768, P, LOW)
         stage2([(6, 0), (6, 1)], LOW, [1, 5])
         multiply(hb2, HALF, 768, P, 3, HIGH)
-        multiply(hb2, HALF, 896, P, 0, LOW)
+        multiply(hb2, HALF, 896, P, 0, (0,))
         quantize_z(768, P, HIGH)
         stage2([(6, 0), (6, 1)], HIGH)
         store(6, 0)
         store(6, 1)
-        multiply(hb2, HALF, 896, P, 1, LOW)
-        multiply(hb2, HALF, 896, P, 2, (2,))
-        quantize_z(896, P, LOW)
-        stage2([(7, 0), (7, 1)], LOW, [6, 3])
-        multiply(hb2, HALF, 896, P, 3, (3,))
-        quantize_z(896, P, (2,))
+        for j in (1, 2, 3):
+            multiply(hb2, HALF, 896, P, j, (j,))
+            quantize_z(896, P, (j - 1,))
+            stage2([(7, 0), (7, 1)], (j - 1,), [6, 4])
         quantize_z(896, P, (3,))
-        stage2([(7, 0), (7, 1)], HIGH)
+        stage2([(7, 0), (7, 1)], (3,))
         store(7, 0)
         store(7, 1, "vector")

@@ -78,10 +78,10 @@ def tile_tensor_feature_core_s4_kernel(tc, x_words, x_scales, u_words, u_scales,
             c_raw[j, oh] = raw
 
         nc.sync.dma_start(out=v_raw[:], in_=v.rearrange("(q p r) j -> p q (r j)", q=4, r=R))
-        uw_raw = sbuf("uw_raw", [P, G, 2 * I], U8)
-        nc.sync.dma_start(out=uw_raw[:].bitcast(I32), in_=u_words.bitcast(I32).rearrange("g p n -> p g n"))
         nc.sync.dma_start(out=b_rows[0:1, :], in_=b.rearrange("(o i) -> o i", o=1))
         load_scales(us_raw, u_scales, 0, I)
+        uw_raw = sbuf("uw_raw", [P, G, 2 * I], U8)
+        nc.sync.dma_start(out=uw_raw[:].bitcast(I32), in_=u_words.bitcast(I32).rearrange("g p n -> p g n"))
         xw_q0 = load_x(0, 256)
         load_scales(xs_first, x_scales, 0, QUARTER)
         load_c(0, 0)
@@ -89,9 +89,11 @@ def tile_tensor_feature_core_s4_kernel(tc, x_words, x_scales, u_words, u_scales,
         load_scales(xs_rest, x_scales, QUARTER, M)
         xw_q1 = load_x(256, 256)
         load_c(2, 0)
-        xw_h1 = load_x(512, 512)
+        xw_q2 = load_x(512, 256)
         load_c(3, 0)
-        for j in range(J):
+        load_c(0, 1)
+        xw_q3 = load_x(768, 256)
+        for j in (1, 2, 3):
             load_c(j, 1)
 
         b_f32 = sbuf("b_f32", [P, T, P], F32)
@@ -113,7 +115,8 @@ def tile_tensor_feature_core_s4_kernel(tc, x_words, x_scales, u_words, u_scales,
             v_bank[q] = vb
 
         spread_v(0, 4)
-        b_bank = bank(7, "b_bank")
+        spread_v(1, 5)
+        b_bank = bank(3, "b_bank")
         for t in range(T):
             nc.tensor.transpose(b_bank[:, t * P : (t + 1) * P], b_f32[:, t, :], ident[:])
         b_col = sbuf("b_col", [P, T], F32)
@@ -121,18 +124,19 @@ def tile_tensor_feature_core_s4_kernel(tc, x_words, x_scales, u_words, u_scales,
 
         uw, us = [], []
         for t in range(T):
-            uw_t = sbuf("uw%d" % t, [P, G, 2 * P], U8)
             us_t = sbuf("us%d" % t, [P, G, P], U8)
-            nc.vector.tensor_copy(
-                out=uw_t[:].bitcast(I32),
-                in_=uw_raw[:].bitcast(I32).rearrange("p g (s t) -> p g s t", t=T)[:, :, :, t],
-            )
             nc.vector.tensor_copy(
                 out=us_t[:].rearrange("p g (s e) -> p g s e", e=E),
                 in_=us_raw[:].rearrange("p g (s t e) -> p g s t e", t=T, e=E)[:, :, :, t, :],
             )
-            uw.append(uw_t)
             us.append(us_t)
+        for t in range(T):
+            uw_t = sbuf("uw%d" % t, [P, G, 2 * P], U8)
+            nc.vector.tensor_copy(
+                out=uw_t[:].bitcast(I32),
+                in_=uw_raw[:].bitcast(I32).rearrange("p g (s t) -> p g s t", t=T)[:, :, :, t],
+            )
+            uw.append(uw_t)
 
         def stage1(acc, t, xw, m0, w, x0=0):
             xs, s0 = (xs_first, m0) if m0 < QUARTER else (xs_rest, m0 - QUARTER)
@@ -166,19 +170,27 @@ def tile_tensor_feature_core_s4_kernel(tc, x_words, x_scales, u_words, u_scales,
         c_stage = {}
         c_codes = {}
 
-        def interleave_c(j, oh, engine, tag=None):
-            stage = sbuf("c_stage%d_%d" % (j, oh), [P, HALF * T], BF16, tag)
-            dst = stage[:].rearrange("p (c i t) -> p c t i", i=RUN, t=T)
-            src = c_raw[j, oh][:].rearrange("p t (c i) -> p c t i", i=RUN)
+        def interleave_c(j, oh, engine, tag=None, cols=(0, HALF)):
+            if (j, oh) not in c_stage:
+                c_stage[j, oh] = sbuf("c_stage%d_%d" % (j, oh), [P, HALF * T], BF16, tag)
+            dst = c_stage[j, oh][:, cols[0] * T : cols[1] * T]
+            src = c_raw[j, oh][:, :, cols[0] : cols[1]]
+            if engine == "gpsimd":
+                nc.gpsimd.tensor_scalar(
+                    out=dst.rearrange("p (c t) -> p c t", t=T),
+                    in0=src.rearrange("p t c -> p c t"),
+                    scalar1=1.0,
+                    scalar2=0.0,
+                    op0=ALU.mult,
+                    op1=ALU.add,
+                )
+                return
+            dst = dst.rearrange("p (c i t) -> p c t i", i=RUN, t=T)
+            src = src.rearrange("p t (c i) -> p c t i", i=RUN)
             if engine == "vector":
                 nc.vector.tensor_copy(out=dst, in_=src)
-            elif engine == "scalar":
-                nc.scalar.copy(out=dst, in_=src)
             else:
-                dst = stage[:].rearrange("p (c t) -> p c t", t=T)
-                src = c_raw[j, oh][:].rearrange("p t c -> p c t")
-                nc.gpsimd.tensor_scalar(out=dst, in0=src, scalar1=1.0, scalar2=0.0, op0=ALU.mult, op1=ALU.add)
-            c_stage[j, oh] = stage
+                nc.scalar.copy(out=dst, in_=src)
 
         def quantize_c(j, oh):
             codes = sbuf("c_codes%d_%d" % (j, oh), [P, HALF], U32)
@@ -232,19 +244,24 @@ def tile_tensor_feature_core_s4_kernel(tc, x_words, x_scales, u_words, u_scales,
                     )
                     y_passes[mt, oh] = done + 1
 
-        def store(mt, oh, engine="scalar"):
-            y = sbuf("y_sb%d_%d" % (mt, oh), [P, HALF], F32)
-            if engine == "scalar":
-                nc.scalar.copy(out=y[:], in_=y_acc[mt, oh][:])
-            else:
-                nc.vector.tensor_copy(out=y[:], in_=y_acc[mt, oh][:])
-            nc.sync.dma_start(out=out[mt * P : (mt + 1) * P, oh * HALF : (oh + 1) * HALF], in_=y[:])
+        def store(mt, oh, engine="scalar", parts=1):
+            w = HALF // parts
+            for n in range(parts):
+                y = sbuf("y_sb%d_%d_%d" % (mt, oh, n), [P, w], F32)
+                acc = y_acc[mt, oh][:, n * w : (n + 1) * w]
+                if engine == "scalar":
+                    nc.scalar.copy(out=y[:], in_=acc)
+                else:
+                    nc.vector.tensor_copy(out=y[:], in_=acc)
+                o0 = oh * HALF + n * w
+                nc.sync.dma_start(out=out[mt * P : (mt + 1) * P, o0 : o0 + w], in_=y[:])
 
         ALL, LOW, HIGH = (0, 1, 2, 3), (0, 1), (2, 3)
         hbA = sbuf("hbA", [P, T, P], F32)
         hbB = sbuf("hbB", [P, T, P], F32)
         hb1 = sbuf("hb1", [P, T, 256], F32)
-        hb2 = sbuf("hb2", [P, T, HALF], F32)
+        hb2 = sbuf("hb2", [P, T, 256], F32)
+        hb3 = sbuf("hb3", [P, T, 256], F32)
 
         hA = stage1_pairs(xw_q0, 0, P, (0, 1))
         hB = stage1_pairs(xw_q0, P, P, (2, 3))
@@ -255,7 +272,8 @@ def tile_tensor_feature_core_s4_kernel(tc, x_words, x_scales, u_words, u_scales,
         bias_vector(hbA, 3, hA[3])
         quantize_c(0, 0)
         interleave_c(2, 0, "gpsimd", "shared_stage")
-        spread_v(1, 5)
+        spread_v(2, 6)
+        spread_v(3, 7)
         h1 = stage1_pairs(xw_q1, 256, 256, (0, 1))
         interleave_c(1, 0, "scalar")
         for t in range(T):
@@ -263,11 +281,7 @@ def tile_tensor_feature_core_s4_kernel(tc, x_words, x_scales, u_words, u_scales,
         for t in range(T):
             bias_scalar(hb1, t, h1[t])
         interleave_c(3, 0, "scalar")
-        h2 = []
-        for t in range(T):
-            acc = bank((6, 7, 2, 3)[t], "h512_%d" % t)
-            stage1(acc[:], t, xw_h1, HALF, HALF)
-            h2.append(acc)
+        h2 = stage1_pairs(xw_q2, 512, 256, (2, 3))
 
         for j in ALL:
             multiply(hbA, 0, 0, P, j, ALL)
@@ -282,62 +296,65 @@ def tile_tensor_feature_core_s4_kernel(tc, x_words, x_scales, u_words, u_scales,
         quantize_c(2, 0)
         interleave_c(0, 1, "gpsimd", "shared_stage")
         stage2([(0, 0), (1, 0)], (3, 2))
-        interleave_c(1, 1, "scalar")
         for t in range(T):
-            bias_scalar(hb2, t, h2[t][:])
-        spread_v(2, 6)
-        spread_v(3, 7)
+            bias_scalar(hb2, t, h2[t])
+        interleave_c(1, 1, "scalar")
+        h3 = stage1_pairs(xw_q3, 768, 256, (2, 3))
         store(0, 0)
         store(1, 0)
+        for t in range(T):
+            bias_scalar(hb3, t, h3[t])
         interleave_c(3, 1, "scalar")
         multiply(hb1, 256, 256, 256, 0, LOW)
         multiply(hb1, 256, 256, 256, 1, LOW)
         multiply(hb1, 256, 256, 256, 2, HIGH)
         quantize_z(256, 256, LOW)
-        stage2([(2, 0), (3, 0)], LOW, [4, 2])
+        stage2([(2, 0), (3, 0)], LOW, [4, 0])
         quantize_c(1, 1)
         quantize_c(0, 1)
-        interleave_c(2, 1, "gpsimd", "shared_stage")
-        stage2([(0, 1), (1, 1), (2, 1)], (1, 0), [3, 0, 1])
+        interleave_c(2, 1, "gpsimd", "shared_stage", (0, 256))
+        interleave_c(2, 1, "scalar", None, (256, HALF))
+        stage2([(0, 1), (1, 1), (2, 1)], (1, 0), [1, 2, 3])
         multiply(hb1, 256, 256, 256, 3, HIGH)
-        multiply(hb2, HALF, 512, 256, 0, LOW)
-        multiply(hb2, HALF, 512, 256, 1, LOW)
+        multiply(hb2, 512, 512, 256, 0, LOW)
         quantize_z(256, 256, HIGH)
         stage2([(3, 1)], LOW, [5])
         stage2([(2, 0), (3, 0)], HIGH)
         store(2, 0)
         store(3, 0)
-        quantize_c(2, 1)
         quantize_c(3, 1)
+        multiply(hb2, 512, 512, 256, 1, LOW)
+        quantize_c(2, 1)
         late = [(mt, 1) for mt in range(4)]
-        stage2(late, HIGH)
+        stage2(late, (3, 2))
         for mt, oh in late:
             store(mt, oh)
         quantize_z(512, 256, LOW)
         third = [(4, 0), (5, 0), (4, 1), (5, 1)]
-        stage2(third, LOW, [4, 2, 3, 0])
-        multiply(hb2, HALF, 512, 256, 2, HIGH)
-        multiply(hb2, HALF, 512, 256, 3, HIGH)
-        multiply(hb2, HALF, 768, P, 0, LOW)
-        quantize_z(512, 256, HIGH)
+        stage2(third, LOW, [4, 0, 1, 2])
+        multiply(hb2, 512, 512, 256, 2, (2,))
+        multiply(hb2, 512, 512, 256, 3, (3,))
+        quantize_z(512, 256, (2,))
+        multiply(hb3, 768, 768, P, 0, LOW)
+        quantize_z(512, 256, (3,))
         stage2(third, HIGH)
         for mt, oh in third:
             store(mt, oh)
-        multiply(hb2, HALF, 768, P, 1, LOW)
-        multiply(hb2, HALF, 768, P, 2, HIGH)
+        multiply(hb3, 768, 768, P, 1, LOW)
+        multiply(hb3, 768, 768, P, 2, HIGH)
         quantize_z(768, P, LOW)
-        stage2([(6, 0), (6, 1)], LOW, [1, 5])
-        multiply(hb2, HALF, 768, P, 3, HIGH)
-        multiply(hb2, HALF, 896, P, 0, (0,))
+        stage2([(6, 0), (6, 1)], LOW, [3, 5])
+        multiply(hb3, 768, 768, P, 3, HIGH)
+        multiply(hb3, 768, 896, P, 0, (0,))
         quantize_z(768, P, HIGH)
         stage2([(6, 0), (6, 1)], HIGH)
         store(6, 0)
         store(6, 1)
         for j in (1, 2, 3):
-            multiply(hb2, HALF, 896, P, j, (j,))
+            multiply(hb3, 768, 896, P, j, (j,))
             quantize_z(896, P, (j - 1,))
             stage2([(7, 0), (7, 1)], (j - 1,), [6, 4])
         quantize_z(896, P, (3,))
         stage2([(7, 0), (7, 1)], (3,))
-        store(7, 0)
-        store(7, 1, "vector")
+        store(7, 0, "scalar", 2)
+        store(7, 1, "vector", 2)

@@ -198,14 +198,33 @@ def tile_tensor_feature_core_s4_kernel(tc, x_words, x_scales, u_words, u_scales,
             nc.vector.quantize_mx(out=codes[:].bitcast(FP8X4), scales=scales[:], in_=c_stage[j, oh][:])
             c_codes[j, oh] = (codes, scales)
 
+        v_last = {}
+
+        def v_to_sbuf(q, m_in_q):
+            row = sbuf("v_last%d" % q, [P, P], F32)
+            vj = v_bank[q][:].bitcast(BF16).rearrange("p (u r c e) -> p u e c r", u=2, r=R, e=2)
+            nc.scalar.copy(
+                out=row[:].rearrange("p (c r) -> p c r", r=R),
+                in_=vj[:, 1, 1, m_in_q // R : (m_in_q + P) // R, :],
+            )
+            v_last[q * QUARTER + m_in_q] = row
+
         z_stage = {}
         z_codes = {}
 
-        def multiply(hb, hb_m0, m0, w, j, group):
+        def multiply(hb, hb_m0, m0, w, j, group, engine="vector", tag=None):
             key = (m0, group[0])
             if key not in z_stage:
-                z_stage[key] = sbuf("z_stage%d_%d" % key, [P, len(group) * w * T], BF16)
+                z_stage[key] = sbuf("z_stage%d_%d" % key, [P, len(group) * w * T], BF16, tag)
             n = j - group[0]
+            if engine == "gpsimd":
+                nc.gpsimd.tensor_tensor(
+                    out=z_stage[key][:, n * w * T : (n + 1) * w * T].rearrange("p (m t) -> p m t", t=T),
+                    in0=hb[:, :, m0 - hb_m0 : m0 - hb_m0 + w].rearrange("p t m -> p m t"),
+                    in1=v_last[m0][:].unsqueeze(2).broadcast_to([P, w, T]),
+                    op=ALU.mult,
+                )
+                return
             dst = z_stage[key][:, n * w * T : (n + 1) * w * T].rearrange("p (c i t) -> p c t i", i=R, t=T)
             src = hb[:, :, m0 - hb_m0 : m0 - hb_m0 + w].rearrange("p t (c i) -> p c t i", i=R)
             c0 = (m0 % QUARTER) // R
@@ -265,28 +284,32 @@ def tile_tensor_feature_core_s4_kernel(tc, x_words, x_scales, u_words, u_scales,
 
         hA = stage1_pairs(xw_q0, 0, P, (0, 1))
         hB = stage1_pairs(xw_q0, P, P, (2, 3))
+        v_to_sbuf(0, 0)
         interleave_c(0, 0, "vector", "shared_stage")
         bias_scalar(hbA, 0, hA[0])
         bias_scalar(hbA, 1, hA[1])
         bias_vector(hbA, 2, hA[2])
         bias_vector(hbA, 3, hA[3])
         quantize_c(0, 0)
+        multiply(hbA, 0, 0, P, 3, ALL, "gpsimd")
         interleave_c(2, 0, "gpsimd", "shared_stage")
         spread_v(2, 6)
         spread_v(3, 7)
         h1 = stage1_pairs(xw_q1, 256, 256, (0, 1))
-        interleave_c(1, 0, "scalar")
+        interleave_c(1, 0, "scalar", None, (0, 256))
         for t in range(T):
             bias_scalar(hbB, t, hB[t])
+        interleave_c(1, 0, "scalar", None, (256, HALF))
         for t in range(T):
             bias_scalar(hb1, t, h1[t])
         interleave_c(3, 0, "scalar")
         h2 = stage1_pairs(xw_q2, 512, 256, (2, 3))
 
-        for j in ALL:
+        for j in (0, 1, 2):
             multiply(hbA, 0, 0, P, j, ALL)
         for j in ALL:
             multiply(hbB, P, P, P, j, ALL)
+        multiply(hb1, 256, 256, 256, 0, LOW)
         quantize_z(0, P, ALL)
         quantize_c(1, 0)
         stage2([(0, 0)], LOW, [0])
@@ -298,6 +321,7 @@ def tile_tensor_feature_core_s4_kernel(tc, x_words, x_scales, u_words, u_scales,
         stage2([(0, 0), (1, 0)], (3, 2))
         for t in range(T):
             bias_scalar(hb2, t, h2[t])
+        v_to_sbuf(3, P)
         interleave_c(1, 1, "scalar")
         h3 = stage1_pairs(xw_q3, 768, 256, (2, 3))
         store(0, 0)
@@ -305,31 +329,30 @@ def tile_tensor_feature_core_s4_kernel(tc, x_words, x_scales, u_words, u_scales,
         for t in range(T):
             bias_scalar(hb3, t, h3[t])
         interleave_c(3, 1, "scalar")
-        multiply(hb1, 256, 256, 256, 0, LOW)
         multiply(hb1, 256, 256, 256, 1, LOW)
         multiply(hb1, 256, 256, 256, 2, HIGH)
+        multiply(hb1, 256, 256, 256, 3, HIGH)
         quantize_z(256, 256, LOW)
         stage2([(2, 0), (3, 0)], LOW, [4, 0])
         quantize_c(1, 1)
+        quantize_z(256, 256, HIGH)
         quantize_c(0, 1)
         interleave_c(2, 1, "gpsimd", "shared_stage", (0, 256))
         interleave_c(2, 1, "scalar", None, (256, HALF))
-        stage2([(0, 1), (1, 1), (2, 1)], (1, 0), [1, 2, 3])
-        multiply(hb1, 256, 256, 256, 3, HIGH)
-        multiply(hb2, 512, 512, 256, 0, LOW)
-        quantize_z(256, 256, HIGH)
-        stage2([(3, 1)], LOW, [5])
         stage2([(2, 0), (3, 0)], HIGH)
         store(2, 0)
         store(3, 0)
-        quantize_c(3, 1)
+        stage2([(0, 1), (1, 1), (2, 1), (3, 1)], (1, 0), [1, 2, 3, 5])
+        multiply(hb2, 512, 512, 256, 0, LOW, "vector", "low_stage")
         multiply(hb2, 512, 512, 256, 1, LOW)
+        quantize_c(3, 1)
         quantize_c(2, 1)
         late = [(mt, 1) for mt in range(4)]
         stage2(late, (3, 2))
         for mt, oh in late:
             store(mt, oh)
         quantize_z(512, 256, LOW)
+        multiply(hb3, 768, 896, P, 3, (3,), "gpsimd", "low_stage")
         third = [(4, 0), (5, 0), (4, 1), (5, 1)]
         stage2(third, LOW, [4, 0, 1, 2])
         multiply(hb2, 512, 512, 256, 2, (2,))
@@ -350,11 +373,13 @@ def tile_tensor_feature_core_s4_kernel(tc, x_words, x_scales, u_words, u_scales,
         stage2([(6, 0), (6, 1)], HIGH)
         store(6, 0)
         store(6, 1)
-        for j in (1, 2, 3):
+        quantize_z(896, P, (3,))
+        stage2([(7, 0), (7, 1)], (3,), [6, 4])
+        for j in (1, 2):
             multiply(hb3, 768, 896, P, j, (j,))
             quantize_z(896, P, (j - 1,))
-            stage2([(7, 0), (7, 1)], (j - 1,), [6, 4])
-        quantize_z(896, P, (3,))
-        stage2([(7, 0), (7, 1)], (3,))
+            stage2([(7, 0), (7, 1)], (j - 1,))
+        quantize_z(896, P, (2,))
+        stage2([(7, 0), (7, 1)], (2,))
         store(7, 0, "scalar", 2)
         store(7, 1, "vector", 2)

from contextlib import ExitStack

import concourse.mybir as mybir
from concourse.masks import make_identity

M, K, I, J, O = 1024, 2048, 512, 4, 1024
FLOPS = 2 * M * K * I + 2 * M * J * I * O

F32 = mybir.dt.float32
BF16 = mybir.dt.bfloat16
I32 = mybir.dt.int32
U32 = mybir.dt.uint32
U8 = mybir.dt.uint8
FP8X4 = mybir.dt.float8_e4m3fn_x4
FP4X4 = mybir.dt.float4_e2m1fn_x4
ALU = mybir.AluOpType
ACT = mybir.ActivationFunctionType

P = 128
G = K // 512
T = 4
HALF = 512
RUN = 4
E = 2
R = 2
QUARTER = 256


def tile_tensor_feature_core_s4_kernel(tc, x_words, x_scales, u_words, u_scales, b, v, core, out):
    nc = tc.nc
    with ExitStack() as ctx:
        sb = ctx.enter_context(tc.tile_pool(name="sb", bufs=1))
        ps = ctx.enter_context(tc.psum_pool(name="ps", bufs=1))
        ctx.enter_context(tc.manual_schedule())

        def sbuf(name, shape, dtype, tag=None):
            return sb.tile(shape, dtype, name=name, tag=tag or name, align_bytes=64)

        def bank(n, name):
            return ps.tile([P, HALF], F32, name=name, tag="bank%d" % n)

        us_raw = sbuf("us_raw", [P, G, I], U8)
        xs_first = sbuf("xs_first", [P, G, QUARTER], U8)
        xs_rest = sbuf("xs_rest", [P, G, M - QUARTER], U8)
        nc.vector.memset(us_raw[:].bitcast(I32), 0)
        nc.vector.memset(xs_first[:].bitcast(I32), 0)
        nc.vector.memset(xs_rest[:].bitcast(I32), 0)

        b_rows = sbuf("b_rows", [P, I], BF16)
        v_raw = sbuf("v_raw", [P, 4, R * J], BF16)
        ident = sbuf("ident", [P, P], F32)
        nc.gpsimd.memset(b_rows[:], 0.0)
        make_identity(nc, ident[:])

        def load_scales(plane, scales, n0, n1):
            rows = scales.bitcast(I32)
            for r in range(4):
                nc.sync.dma_start(
                    out=plane[r:P:32].bitcast(I32),
                    in_=rows[:, r:16:4, n0 // 4 : n1 // 4].rearrange("g q n -> q g n"),
                )

        def load_x(m0, w):
            xw = sbuf("xw%d" % m0, [P, G, 2 * w], U8)
            nc.sync.dma_start(
                out=xw[:].bitcast(I32),
                in_=x_words.bitcast(I32)[:, :, m0 // 2 : (m0 + w) // 2].rearrange("g p n -> p g n"),
            )
            return xw

        c_raw = {}

        def load_c(j, oh):
            raw = sbuf("c_raw%d_%d" % (j, oh), [P, T, HALF], BF16)
            rows = core[j].rearrange("(s t e) o -> e s t o", t=T, e=E)
            for e in range(E):
                nc.sync.dma_start(out=raw[e:P:E], in_=rows[e][:, :, oh * HALF : (oh + 1) * HALF])
            c_raw[j, oh] = raw

        nc.sync.dma_start(out=v_raw[:], in_=v.rearrange("(q p r) j -> p q (r j)", q=4, r=R))
        nc.sync.dma_start(out=b_rows[0:1, :], in_=b.rearrange("(o i) -> o i", o=1))
        load_scales(us_raw, u_scales, 0, I)
        uw_raw = sbuf("uw_raw", [P, G, 2 * I], U8)
        nc.sync.dma_start(out=uw_raw[:].bitcast(I32), in_=u_words.bitcast(I32).rearrange("g p n -> p g n"))
        xw_q0 = load_x(0, 256)
        load_scales(xs_first, x_scales, 0, QUARTER)
        load_c(0, 0)
        load_c(1, 0)
        load_scales(xs_rest, x_scales, QUARTER, M)
        xw_q1 = load_x(256, 256)
        load_c(2, 0)
        xw_q2 = load_x(512, 256)
        load_c(3, 0)
        load_c(0, 1)
        xw_q3 = load_x(768, 256)
        for j in (1, 2, 3):
            load_c(j, 1)

        b_f32 = sbuf("b_f32", [P, T, P], F32)
        nc.scalar.activation(
            out=b_f32[:].rearrange("p t (s e) -> p t s e", e=E),
            in_=b_rows[:].rearrange("p (s t e) -> p t s e", t=T, e=E),
            func=ACT.Identity,
        )
        v_words = v_raw[:].bitcast(F32)
        v_bank = {}

        def spread_v(q, n):
            vb = bank(n, "v%d" % q)
            for u in range(2):
                for r in range(R):
                    col = v_words[:, q, 2 * r + u : 2 * r + u + 1]
                    slot = R * u + r
                    nc.tensor.transpose(vb[:, slot * P : (slot + 1) * P], col.to_broadcast([P, P]), ident[:])
            v_bank[q] = vb

        spread_v(0, 4)
        spread_v(1, 5)
        b_bank = bank(3, "b_bank")
        for t in range(T):
            nc.tensor.transpose(b_bank[:, t * P : (t + 1) * P], b_f32[:, t, :], ident[:])
        b_col = sbuf("b_col", [P, T], F32)
        nc.scalar.copy(out=b_col[:], in_=b_bank[:].rearrange("p (t n) -> p t n", t=T)[:, :, 0])

        uw, us = [], []
        for t in range(T):
            us_t = sbuf("us%d" % t, [P, G, P], U8)
            nc.vector.tensor_copy(
                out=us_t[:].rearrange("p g (s e) -> p g s e", e=E),
                in_=us_raw[:].rearrange("p g (s t e) -> p g s t e", t=T, e=E)[:, :, :, t, :],
            )
            us.append(us_t)
        for t in range(T):
            uw_t = sbuf("uw%d" % t, [P, G, 2 * P], U8)
            nc.vector.tensor_copy(
                out=uw_t[:].bitcast(I32),
                in_=uw_raw[:].bitcast(I32).rearrange("p g (s t) -> p g s t", t=T)[:, :, :, t],
            )
            uw.append(uw_t)

        def stage1(acc, t, xw, m0, w, x0=0):
            xs, s0 = (xs_first, m0) if m0 < QUARTER else (xs_rest, m0 - QUARTER)
            for g in range(G):
                nc.tensor.matmul_mx(
                    out=acc,
                    lhsT=uw[t][:, g, :].bitcast(FP4X4),
                    lhsT_scale=us[t][:, g, :],
                    rhs=xw[:, g, 2 * x0 : 2 * (x0 + w)].bitcast(FP4X4),
                    rhs_scale=xs[:, g, s0 : s0 + w],
                    start=(g == 0),
                    stop=(g == G - 1),
                )

        def stage1_pairs(xw, m0, w, banks):
            accs = []
            for half in range(2):
                pair = bank(banks[half], "h%d_%d" % (m0, half))
                for tt in range(2):
                    acc = pair[:, tt * w : (tt + 1) * w]
                    stage1(acc, 2 * half + tt, xw, m0, w, m0 % QUARTER)
                    accs.append(acc)
            return accs

        def bias_vector(hb, t, acc):
            nc.vector.tensor_scalar(out=hb[:, t, :], in0=acc, scalar1=b_col[:, t : t + 1], scalar2=None, op0=ALU.add)

        def bias_scalar(hb, t, acc):
            nc.scalar.activation(out=hb[:, t, :], in_=acc, func=ACT.Identity, bias=b_col[:, t : t + 1])

        c_stage = {}
        c_codes = {}

        def interleave_c(j, oh, engine, tag=None, cols=(0, HALF)):
            if (j, oh) not in c_stage:
                c_stage[j, oh] = sbuf("c_stage%d_%d" % (j, oh), [P, HALF * T], BF16, tag)
            dst = c_stage[j, oh][:, cols[0] * T : cols[1] * T]
            src = c_raw[j, oh][:, :, cols[0] : cols[1]]
            if engine == "gpsimd":
                nc.gpsimd.tensor_scalar(
                    out=dst.rearrange("p (c t) -> p c t", t=T),
                    in0=src.rearrange("p t c -> p c t"),
                    scalar1=1.0,
                    scalar2=0.0,
                    op0=ALU.mult,
                    op1=ALU.add,
                )
                return
            dst = dst.rearrange("p (c i t) -> p c t i", i=RUN, t=T)
            src = src.rearrange("p t (c i) -> p c t i", i=RUN)
            if engine == "vector":
                nc.vector.tensor_copy(out=dst, in_=src)
            else:
                nc.scalar.copy(out=dst, in_=src)

        def quantize_c(j, oh):
            codes = sbuf("c_codes%d_%d" % (j, oh), [P, HALF], U32)
            scales = sbuf("c_scales%d_%d" % (j, oh), [P, HALF], U8)
            nc.vector.quantize_mx(out=codes[:].bitcast(FP8X4), scales=scales[:], in_=c_stage[j, oh][:])
            c_codes[j, oh] = (codes, scales)

        v_last = {}

        def v_to_sbuf(q, m_in_q):
            row = sbuf("v_last%d" % q, [P, P], F32)
            vj = v_bank[q][:].bitcast(BF16).rearrange("p (u r c e) -> p u e c r", u=2, r=R, e=2)
            nc.scalar.copy(
                out=row[:].rearrange("p (c r) -> p c r", r=R),
                in_=vj[:, 1, 1, m_in_q // R : (m_in_q + P) // R, :],
            )
            v_last[q * QUARTER + m_in_q] = row

        z_stage = {}
        z_codes = {}

        def multiply(hb, hb_m0, m0, w, j, group, engine="vector", tag=None):
            key = (m0, group[0])
            if key not in z_stage:
                z_stage[key] = sbuf("z_stage%d_%d" % key, [P, len(group) * w * T], BF16, tag)
            n = j - group[0]
            if engine == "gpsimd":
                nc.gpsimd.tensor_tensor(
                    out=z_stage[key][:, n * w * T : (n + 1) * w * T].rearrange("p (m t) -> p m t", t=T),
                    in0=hb[:, :, m0 - hb_m0 : m0 - hb_m0 + w].rearrange("p t m -> p m t"),
                    in1=v_last[m0][:].unsqueeze(2).broadcast_to([P, w, T]),
                    op=ALU.mult,
                )
                return
            dst = z_stage[key][:, n * w * T : (n + 1) * w * T].rearrange("p (c i t) -> p c t i", i=R, t=T)
            src = hb[:, :, m0 - hb_m0 : m0 - hb_m0 + w].rearrange("p t (c i) -> p c t i", i=R)
            c0 = (m0 % QUARTER) // R
            vj = v_bank[m0 // QUARTER][:].bitcast(BF16).rearrange("p (u r c e) -> p u c e r", u=2, r=R, e=2)
            vj = vj[:, j // 2, c0 : c0 + w // R, j % 2 : j % 2 + 1, :].broadcast_to([P, w // R, T, R])
            nc.vector.tensor_tensor(out=dst, in0=src, in1=vj, op=ALU.mult)

        def quantize_z(m0, w, group):
            key = (m0, group[0])
            codes = sbuf("z_codes%d_%d" % key, [P, len(group) * w], U32)
            scales = sbuf("z_scales%d_%d" % key, [P, len(group) * w], U8)
            nc.vector.quantize_mx(out=codes[:].bitcast(FP8X4), scales=scales[:], in_=z_stage[key][:])
            for n, j in enumerate(group):
                for a in range(w // P):
                    cols = slice(n * w + a * P, n * w + (a + 1) * P)
                    z_codes[m0 // P + a, j] = (codes[:, cols], scales[:, cols])

        y_acc = {}
        y_passes = {}

        def stage2(groups, js, banks=()):
            for j in js:
                for n, (mt, oh) in enumerate(groups):
                    if (mt, oh) not in y_acc:
                        y_acc[mt, oh] = bank(banks[n], "y%d_%d" % (mt, oh))
                        y_passes[mt, oh] = 0
                    done = y_passes[mt, oh]
                    nc.tensor.matmul_mx(
                        out=y_acc[mt, oh][:],
                        lhsT=z_codes[mt, j][0].bitcast(FP8X4),
                        lhsT_scale=z_codes[mt, j][1],
                        rhs=c_codes[j, oh][0][:].bitcast(FP8X4),
                        rhs_scale=c_codes[j, oh][1][:],
                        start=(done == 0),
                        stop=(done == J - 1),
                    )
                    y_passes[mt, oh] = done + 1

        def store(mt, oh, engine="scalar", parts=1):
            w = HALF // parts
            for n in range(parts):
                y = sbuf("y_sb%d_%d_%d" % (mt, oh, n), [P, w], F32)
                acc = y_acc[mt, oh][:, n * w : (n + 1) * w]
                if engine == "scalar":
                    nc.scalar.copy(out=y[:], in_=acc)
                else:
                    nc.vector.tensor_copy(out=y[:], in_=acc)
                o0 = oh * HALF + n * w
                nc.sync.dma_start(out=out[mt * P : (mt + 1) * P, o0 : o0 + w], in_=y[:])

        ALL, LOW, HIGH = (0, 1, 2, 3), (0, 1), (2, 3)
        hbA = sbuf("hbA", [P, T, P], F32)
        hbB = sbuf("hbB", [P, T, P], F32)
        hb1 = sbuf("hb1", [P, T, 256], F32)
        hb2 = sbuf("hb2", [P, T, 256], F32)
        hb3 = sbuf("hb3", [P, T, 256], F32)

        hA = stage1_pairs(xw_q0, 0, P, (0, 1))
        hB = stage1_pairs(xw_q0, P, P, (2, 3))
        v_to_sbuf(0, 0)
        interleave_c(0, 0, "vector", "shared_stage")
        bias_scalar(hbA, 0, hA[0])
        bias_scalar(hbA, 1, hA[1])
        bias_vector(hbA, 2, hA[2])
        bias_vector(hbA, 3, hA[3])
        quantize_c(0, 0)
        multiply(hbA, 0, 0, P, 3, ALL, "gpsimd")
        interleave_c(2, 0, "gpsimd", "shared_stage")
        spread_v(2, 6)
        spread_v(3, 7)
        h1 = stage1_pairs(xw_q1, 256, 256, (0, 1))
        interleave_c(1, 0, "scalar", None, (0, 256))
        for t in range(T):
            bias_scalar(hbB, t, hB[t])
        interleave_c(1, 0, "scalar", None, (256, HALF))
        for t in range(T):
            bias_scalar(hb1, t, h1[t])
        interleave_c(3, 0, "scalar")
        h2 = stage1_pairs(xw_q2, 512, 256, (2, 3))

        for j in (0, 1, 2):
            multiply(hbA, 0, 0, P, j, ALL)
        for j in ALL:
            multiply(hbB, P, P, P, j, ALL)
        multiply(hb1, 256, 256, 256, 0, LOW)
        quantize_z(0, P, ALL)
        quantize_c(1, 0)
        stage2([(0, 0)], LOW, [0])
        quantize_z(P, P, ALL)
        stage2([(1, 0)], LOW, [1])
        quantize_c(3, 0)
        quantize_c(2, 0)
        interleave_c(0, 1, "gpsimd", "shared_stage")
        stage2([(0, 0), (1, 0)], (3, 2))
        for t in range(T):
            bias_scalar(hb2, t, h2[t])
        v_to_sbuf(3, P)
        interleave_c(1, 1, "scalar")
        h3 = stage1_pairs(xw_q3, 768, 256, (2, 3))
        store(0, 0)
        store(1, 0)
        for t in range(T):
            bias_scalar(hb3, t, h3[t])
        interleave_c(3, 1, "scalar")
        multiply(hb1, 256, 256, 256, 1, LOW)
        multiply(hb1, 256, 256, 256, 2, HIGH)
        multiply(hb1, 256, 256, 256, 3, HIGH)
        quantize_z(256, 256, LOW)
        stage2([(2, 0), (3, 0)], LOW, [4, 0])
        quantize_c(1, 1)
        quantize_z(256, 256, HIGH)
        quantize_c(0, 1)
        interleave_c(2, 1, "gpsimd", "shared_stage", (0, 256))
        interleave_c(2, 1, "scalar", None, (256, HALF))
        stage2([(2, 0), (3, 0)], HIGH)
        store(2, 0)
        store(3, 0)
        stage2([(0, 1), (1, 1), (2, 1), (3, 1)], (1, 0), [1, 2, 3, 5])
        multiply(hb2, 512, 512, 256, 0, LOW, "vector", "low_stage")
        multiply(hb2, 512, 512, 256, 1, LOW)
        quantize_c(3, 1)
        quantize_c(2, 1)
        late = [(mt, 1) for mt in range(4)]
        stage2(late, (3, 2))
        for mt, oh in late:
            store(mt, oh)
        quantize_z(512, 256, LOW)
        multiply(hb3, 768, 896, P, 3, (3,), "gpsimd", "low_stage")
        third = [(4, 0), (5, 0), (4, 1), (5, 1)]
        stage2(third, LOW, [4, 0, 1, 2])
        multiply(hb2, 512, 512, 256, 2, (2,))
        multiply(hb2, 512, 512, 256, 3, (3,))
        quantize_z(512, 256, (2,))
        multiply(hb3, 768, 768, P, 0, LOW)
        quantize_z(512, 256, (3,))
        stage2(third, HIGH)
        for mt, oh in third:
            store(mt, oh)
        multiply(hb3, 768, 768, P, 1, LOW)
        multiply(hb3, 768, 768, P, 2, HIGH)
        quantize_z(768, P, LOW)
        stage2([(6, 0), (6, 1)], LOW, [3, 5])
        multiply(hb3, 768, 768, P, 3, HIGH)
        multiply(hb3, 768, 896, P, 0, (0,))
        quantize_z(768, P, HIGH)
        stage2([(6, 0), (6, 1)], HIGH)
        store(6, 0)
        store(6, 1)
        quantize_z(896, P, (3,))
        stage2([(7, 0), (7, 1)], (3,), [6, 4])
        for j in (1, 2):
            multiply(hb3, 768, 896, P, j, (j,))
            quantize_z(896, P, (j - 1,))
            stage2([(7, 0), (7, 1)], (j - 1,))
        quantize_z(896, P, (2,))
        stage2([(7, 0), (7, 1)], (2,))
        store(7, 0, "scalar", 2)
        store(7, 1, "vector", 2)
